import numpy as np
import ml_dtypes


def mxq(x, axis, fmt="e4m3"):
    dtype, down = {"e4m3": (ml_dtypes.float8_e4m3fn, 7), "e5m2": (ml_dtypes.float8_e5m2, 14)}[fmt]
    v = np.moveaxis(np.asarray(x, np.float32).astype(ml_dtypes.bfloat16).astype(np.float64), axis, -1)
    blocks = v.reshape(v.shape[:-1] + (-1, 32))
    amax = np.abs(blocks).max(-1, keepdims=True)
    byte = np.maximum(np.where(amax > 0, np.frexp(amax)[1] - 1 + 127, 0) - down, 1)
    scale = np.exp2(byte - 127.0)
    codes = (blocks / scale).astype(np.float32).astype(dtype).astype(np.float64)
    return np.moveaxis((codes * scale).reshape(v.shape), -1, axis)


WIDE = False


def mx_kscale(k):
    if not WIDE:
        return np.ones(k)
    levels = np.array([10, -10, 5, -5, 0])
    if k % 512:
        return np.exp2(np.random.permutation(np.resize(levels, k // 32))).repeat(32)
    a = np.empty((k // 512, 16))
    for p in range(k // 512):
        a[p, :8] = np.random.permutation(np.resize(levels, 8))
        for g in range(8):
            far = levels[np.abs(levels - a[p, g]) >= 10]
            a[p, g + 8] = far[np.random.randint(len(far))]
    return np.exp2(a.ravel()).repeat(32)


def f64(x):
    return np.asarray(x).astype(np.float64)


def striped(idx):
    return np.tile(idx.reshape(-1, 16).T, (8, 1)).astype(np.uint16)


def unstriped(offs):
    return offs[:16].T.reshape(-1).astype(np.int64)


def striped8(idx):
    return np.concatenate([v.reshape(-1, 16).T for v in idx]).astype(np.uint16)


def unstriped8(offs):
    return np.stack([offs[16 * g:16 * g + 16].T.reshape(-1) for g in range(8)]).astype(np.int64)


E2M1 = np.array([0.0, 0.5, 1.0, 1.5, 2.0, 3.0, 4.0, 6.0, -0.0, -0.5, -1.0, -1.5, -2.0, -3.0, -4.0, -6.0])


def pack_weight(w, fmt):
    k, n = w.shape
    w = f64(np.asarray(w, np.float32).astype(ml_dtypes.bfloat16)).reshape(k // 32, 32, n)
    amax = np.abs(w).max(1)
    if fmt == "e4m3":
        byte = np.frexp(amax)[1] - 1 + 127 - 7
    else:
        mant, ex = np.frexp(amax / 6.0)
        byte = np.where(mant > 0.5, ex, ex - 1) + 127
    byte = np.clip(np.where(amax > 0, byte, 1), 1, 254)
    scaled = (w * np.exp2(127.0 - byte)[:, None, :]).reshape(k, n).astype(np.float32)
    by_word = np.ascontiguousarray(scaled.reshape(k // 512, 128, 4, n).transpose(0, 1, 3, 2))
    if fmt == "e4m3":
        words = by_word.astype(ml_dtypes.float8_e4m3fn).view(np.uint8)
    else:
        c = by_word.astype(ml_dtypes.float4_e2m1fn).view(np.uint8) & 0xF
        words = (c[..., 0::2] | (c[..., 1::2] << 4)).reshape(k // 512, 128, 2 * n)
    return np.ascontiguousarray(words), np.ascontiguousarray(byte.astype(np.uint8).reshape(k // 512, 16, n))


def unpack_weight(words, scales, fmt):
    g, _, n = scales.shape
    words = np.ascontiguousarray(words).reshape(g, 128, n, -1)
    if fmt == "e4m3":
        vals = words.view(ml_dtypes.float8_e4m3fn).astype(np.float64)
    else:
        nib = np.empty((g, 128, n, 4), np.uint8)
        nib[..., 0::2] = words & 0xF
        nib[..., 1::2] = words >> 4
        vals = E2M1[nib]
    vals = vals * np.repeat(np.exp2(scales.astype(np.float64) - 127.0), 8, axis=1)[..., None]
    return vals.transpose(0, 1, 3, 2).reshape(g * 512, n)


def pack_table(v):
    words, scales = pack_weight(v, "e4m3")
    return np.concatenate([words.reshape(words.shape[0], -1), scales.reshape(scales.shape[0], -1)], axis=1)


def unpack_table(tab):
    g, t = tab.shape[0], tab.shape[1] // 528
    return unpack_weight(tab[:, :512 * t].reshape(g, 128, t, 4), tab[:, 512 * t:].reshape(g, 16, t), "e4m3")


def gelu(v):
    return 0.5 * v * (1.0 + np.tanh(np.sqrt(2.0 / np.pi) * (v + 0.044715 * v**3)))


K, L, M, T, S = 1024, 1536, 128, 1024, 512


def setup_inputs():
    n = np.random.standard_normal
    s1 = mx_kscale(K)[:, None]
    s2 = mx_kscale(L)[:, None]
    p_w4 = pack_weight(n((K, M)) / np.sqrt(K) / s1, "e2m1")
    return {
        "xT": (n((K, T)) * s1).astype(np.float32),
        "w4_words": p_w4[0],
        "w4_scales": p_w4[1],
        "tab": pack_table(n((L, T)) * s2),
        "u": (n((L, M)) / np.sqrt(L) / s2).astype(np.float32),
        "wgt": np.repeat(np.random.uniform(0.5, 2.0, (8, S)), 16, axis=0).astype(np.float32),
        "b": (0.3 * n(128)).astype(np.float32),
        "offs": striped(np.random.permutation(T)[:S]),
        "offs2": striped8(np.stack([np.random.permutation(T)[:S] for _ in range(8)])),
    }


def reference(xT, w4_words, w4_scales, tab, u, wgt, b, offs, offs2):
    idx2 = unstriped8(offs2)
    group = np.arange(K) % 512 // 64
    xg = f64(wgt)[np.arange(K) // 4 % 128] * f64(xT)[np.arange(K)[:, None], idx2[group]]
    xT_ = mxq(xg, 0, "e4m3")
    w4_ = unpack_weight(w4_words, w4_scales, "e2m1")
    tab_ = unpack_table(tab)[:, unstriped(offs)]
    u_ = mxq(f64(u), 0, "e4m3")
    y = xT_.T @ w4_ + tab_.T @ u_
    return gelu(y + f64(b)[None, :])

@@ -1,0 +1,178 @@
+from contextlib import ExitStack
+
+import concourse.mybir as mybir
+from concourse.masks import make_identity
+
+K, L, M, T, S = 1024, 1536, 128, 1024, 512
+FLOPS = 2 * S * M * (K + L)
+
+F32 = mybir.dt.float32
+BF16 = mybir.dt.bfloat16
+I32 = mybir.dt.int32
+U32 = mybir.dt.uint32
+U16 = mybir.dt.uint16
+U8 = mybir.dt.uint8
+FP8X4 = mybir.dt.float8_e4m3fn_x4
+FP4X4 = mybir.dt.float4_e2m1fn_x4
+MULT = mybir.AluOpType.mult
+ADD = mybir.AluOpType.add
+GELU = mybir.ActivationFunctionType.Gelu_apprx_tanh
+
+P = 128
+PACK = 4
+X_PASSES = K // (P * PACK)
+V_PASSES = L // (P * PACK)
+ROW_TILES = S // P
+QUADS = 4
+
+
+def tile_list_htab_tm_gelu_kernel(tc, xT, w4_words, w4_scales, tab, u, wgt, b, offs, offs2, out):
+    nc = tc.nc
+    with ExitStack() as ctx:
+        sb = ctx.enter_context(tc.tile_pool(name="sb", bufs=1))
+        ps = ctx.enter_context(tc.psum_pool(name="ps", bufs=1))
+
+        list_v = sb.tile([P, S // 16], U16, name="list_v")
+        list_x = sb.tile([P, S // 16], U16, name="list_x")
+        wgt_sb = sb.tile([P, S], F32, name="wgt_sb")
+        x_sb = [[sb.tile([P, T], F32, name=f"x_sb{a}_{i}") for i in range(PACK)] for a in range(X_PASSES)]
+        v_words = [sb.tile([P, T], I32, name=f"v_words{a}", tag=f"v_words{a}", align_bytes=64) for a in range(V_PASSES)]
+        v_scales = sb.tile([P, T], U8, name="v_scales")
+        w_words = sb.tile([P, X_PASSES, 2 * M], U8, name="w_words", align_bytes=64)
+        w_scales = sb.tile([P, X_PASSES, M], U8, name="w_scales", align_bytes=64)
+        u_sb = [sb.tile([P, PACK, M], F32, name=f"u_sb{a}") for a in range(V_PASSES)]
+        b_col = sb.tile([P, 1], F32, name="b_col")
+        ident = sb.tile([P, P], F32, name="ident")
+
+        nc.vector.memset(v_scales[:].bitcast(I32), 0)
+        nc.vector.memset(w_scales[:].rearrange("p a n -> p (a n)").bitcast(I32), 0)
+        make_identity(nc, ident[:])
+
+        x_planes = xT.rearrange("(a p i) t -> a i p t", p=P, i=PACK)
+        tab_scales = tab[:, PACK * P * T :].rearrange("a (q t) -> a q t", t=T)
+
+        nc.sync.dma_start(list_x[:], offs2)
+        nc.sync.dma_start(wgt_sb[:], wgt)
+        nc.sync.dma_start(x_sb[0][0][:], x_planes[0, 0])
+        nc.sync.dma_start(x_sb[0][1][:], x_planes[0, 1])
+        nc.sync.dma_start(list_v[:], offs)
+        for q in range(QUADS):
+            nc.scalar.dma_start(
+                v_scales[32 * q : 32 * q + 4 * V_PASSES, :].bitcast(I32),
+                tab_scales[:, 4 * q : 4 * q + 4, :].bitcast(I32),
+            )
+        for q in range(QUADS):
+            nc.scalar.dma_start(
+                w_scales[32 * q : 32 * q + 4, :, :].bitcast(I32),
+                w4_scales[:, 4 * q : 4 * q + 4, :].rearrange("a r n -> r a n").bitcast(I32),
+            )
+        nc.scalar.dma_start(w_words[:].bitcast(I32), w4_words.rearrange("a p c -> p a c").bitcast(I32))
+        with nc.allow_non_contiguous_dma(reason="one bias value a partition"):
+            nc.scalar.dma_start(b_col[:], b.rearrange("(p o) -> p o", o=1))
+        nc.sync.dma_start(x_sb[0][2][:], x_planes[0, 2])
+        nc.sync.dma_start(x_sb[0][3][:], x_planes[0, 3])
+        u_passes = u.rearrange("(a p i) n -> a p (i n)", p=P, i=PACK)
+        for i in range(PACK):
+            nc.sync.dma_start(x_sb[1][i][:], x_planes[1, i])
+            if i < V_PASSES:
+                nc.sync.dma_start(u_sb[i][:].rearrange("p i n -> p (i n)"), u_passes[i])
+        for a in range(V_PASSES):
+            nc.sync.dma_start(v_words[a][:], tab[a, 0 : PACK * P * T].rearrange("(p c) -> p c", p=P).bitcast(I32))
+
+        acc = [ps.tile([P, M], F32, name=f"acc{t}") for t in range(ROW_TILES)]
+
+        x_codes = []
+        x_scales = []
+        wovens = []
+
+        def quantize_x(a, tag):
+            codes = sb.tile([P, S], U32, name=f"x_codes{a}", tag=tag, align_bytes=64)
+            scales = sb.tile([P, S], U8, name=f"x_scales{a}", align_bytes=64)
+            nc.vector.quantize_mx(out=codes[:].bitcast(FP8X4), scales=scales[:], in_=wovens[a][:].rearrange("p j i -> p (j i)"))
+            x_codes.append(codes)
+            x_scales.append(scales)
+
+        for a in range(X_PASSES):
+            picked = sb.tile([P, PACK, S], F32, name=f"picked{a}")
+            for i in range(PACK):
+                nc.vector.tensor_tensor(picked[:, i, :], x_sb[a][i][:].indirect(list_x[:]), wgt_sb[:], MULT)
+            woven = sb.tile([P, S, PACK], BF16, name=f"woven{a}", align_bytes=64)
+            nc.scalar.copy(
+                woven[:].rearrange("p (c e) i -> p c i e", e=4),
+                picked[:].rearrange("p i (c e) -> p c i e", e=4),
+            )
+            wovens.append(woven)
+            if a == 0:
+                quantize_x(a, "x_codes0")
+
+        b_ps = ps.tile([P, M], F32, name="b_ps")
+        nc.tensor.transpose(b_ps[:], b_col[:].to_broadcast([P, P]), ident[:])
+        b_rows = sb.tile([P, M], F32, name="b_rows")
+        nc.scalar.copy(b_rows[:], b_ps[:])
+
+        u_woven = sb.tile([P, V_PASSES, M, PACK], BF16, name="u_woven", align_bytes=64)
+        u_codes = sb.tile([P, V_PASSES, M], U32, name="u_codes", align_bytes=64)
+        u_scales = sb.tile([P, V_PASSES, M], U8, name="u_scales", align_bytes=64)
+        for a in range(V_PASSES):
+            nc.scalar.copy(
+                u_woven[:, a].rearrange("p (c e) i -> p c i e", e=4),
+                u_sb[a][:].rearrange("p i (c e) -> p c i e", e=4),
+            )
+        for lo, hi in ((0, 2), (2, 3)):
+            nc.vector.quantize_mx(
+                out=u_codes[:, lo:hi, :].rearrange("p a n -> p (a n)").bitcast(FP8X4),
+                scales=u_scales[:, lo:hi, :].rearrange("p a n -> p (a n)"),
+                in_=u_woven[:, lo:hi].rearrange("p a n i -> p (a n i)"),
+            )
+
+        g_scales = sb.tile([P, S], U8, name="g_scales", align_bytes=64)
+        nc.vector.tensor_copy(g_scales[:], v_scales[:].indirect(list_v[:]))
+        g_words = [sb.tile([P, S], U32, name=f"g_words{a}", align_bytes=64) for a in range(V_PASSES)]
+        for a in range(V_PASSES - 1):
+            nc.vector.tensor_copy(g_words[a][:], v_words[a][:].bitcast(U32).indirect(list_v[:]))
+        quantize_x(1, "v_words1")
+        last = V_PASSES - 1
+        for t in range(ROW_TILES):
+            nc.vector.tensor_copy(
+                g_words[last][:, P * t : P * (t + 1)],
+                v_words[last][:].bitcast(U32).indirect(list_v[:, 8 * t : 8 * (t + 1)]),
+            )
+
+        def x_pass(a, start):
+            for t in range(ROW_TILES):
+                rows = slice(P * t, P * (t + 1))
+                nc.tensor.matmul_mx(
+                    out=acc[t][:],
+                    lhsT=x_codes[a][:, rows].bitcast(FP8X4),
+                    lhsT_scale=x_scales[a][:, rows],
+                    rhs=w_words[:, a, :].bitcast(FP4X4),
+                    rhs_scale=w_scales[:, a, :],
+                    start=start,
+                    stop=False,
+                )
+
+        def v_pass(a):
+            for t in range(ROW_TILES):
+                rows = slice(P * t, P * (t + 1))
+                nc.tensor.matmul_mx(
+                    out=acc[t][:],
+                    lhsT=g_words[a][:, rows].bitcast(FP8X4),
+                    lhsT_scale=g_scales[4 * a : P, rows],
+                    rhs=u_codes[:, a, :].bitcast(FP8X4),
+                    rhs_scale=u_scales[:, a, :],
+                    start=False,
+                    stop=(a == last),
+                )
+
+        x_pass(0, True)
+        v_pass(0)
+        v_pass(1)
+        x_pass(1, False)
+        v_pass(2)
+
+        for t in range(ROW_TILES):
+            summed = sb.tile([P, M], F32, name=f"summed{t}")
+            nc.vector.tensor_tensor(summed[:], acc[t][:], b_rows[:], ADD)
+            result = sb.tile([P, M], F32, name=f"result{t}")
+            nc.scalar.activation(result[:], summed[:], GELU)
+            nc.sync.dma_start(out[P * t : P * (t + 1), :], result[:])

@@ -16,6 +16,7 @@ FP8X4 = mybir.dt.float8_e4m3fn_x4
 FP4X4 = mybir.dt.float4_e2m1fn_x4
 MULT = mybir.AluOpType.mult
 ADD = mybir.AluOpType.add
+COPY = mybir.ActivationFunctionType.Copy
 GELU = mybir.ActivationFunctionType.Gelu_apprx_tanh
 
 P = 128
@@ -35,7 +36,7 @@ def tile_list_htab_tm_gelu_kernel(tc, xT, w4_words, w4_scales, tab, u, wgt, b, o
         list_v = sb.tile([P, S // 16], U16, name="list_v")
         list_x = sb.tile([P, S // 16], U16, name="list_x")
         wgt_sb = sb.tile([P, S], F32, name="wgt_sb")
-        x_sb = [[sb.tile([P, T], F32, name=f"x_sb{a}_{i}") for i in range(PACK)] for a in range(X_PASSES)]
+        x_sb = [[sb.tile([P, T], F32, name=f"x_sb{a}_{i}", tag=f"x_sb{a}_{i}", align_bytes=64) for i in range(PACK)] for a in range(X_PASSES)]
         v_words = [sb.tile([P, T], I32, name=f"v_words{a}", tag=f"v_words{a}", align_bytes=64) for a in range(V_PASSES)]
         v_scales = sb.tile([P, T], U8, name="v_scales")
         w_words = sb.tile([P, X_PASSES, 2 * M], U8, name="w_words", align_bytes=64)
@@ -44,99 +45,127 @@ def tile_list_htab_tm_gelu_kernel(tc, xT, w4_words, w4_scales, tab, u, wgt, b, o
         b_col = sb.tile([P, 1], F32, name="b_col")
         ident = sb.tile([P, P], F32, name="ident")
 
+        make_identity(nc, ident[:])
         nc.vector.memset(v_scales[:].bitcast(I32), 0)
         nc.vector.memset(w_scales[:].rearrange("p a n -> p (a n)").bitcast(I32), 0)
-        make_identity(nc, ident[:])
 
         x_planes = xT.rearrange("(a p i) t -> a i p t", p=P, i=PACK)
         tab_scales = tab[:, PACK * P * T :].rearrange("a (q t) -> a q t", t=T)
+        u_passes = u.rearrange("(a p i) n -> a p (i n)", p=P, i=PACK)
 
-        nc.sync.dma_start(list_x[:], offs2)
-        nc.sync.dma_start(wgt_sb[:], wgt)
-        nc.sync.dma_start(x_sb[0][0][:], x_planes[0, 0])
-        nc.sync.dma_start(x_sb[0][1][:], x_planes[0, 1])
-        nc.sync.dma_start(list_v[:], offs)
-        for q in range(QUADS):
-            nc.scalar.dma_start(
+        def load_u(a):
+            nc.sync.dma_start(u_sb[a][:].rearrange("p i n -> p (i n)"), u_passes[a])
+
+        def load_v(a):
+            nc.sync.dma_start(v_words[a][:], tab[a, 0 : PACK * P * T].rearrange("(p c) -> p c", p=P).bitcast(I32))
+
+        def load_x(a, i):
+            nc.sync.dma_start(x_sb[a][i][:], x_planes[a, i])
+
+        def load_v_scales(q):
+            nc.sync.dma_start(
                 v_scales[32 * q : 32 * q + 4 * V_PASSES, :].bitcast(I32),
                 tab_scales[:, 4 * q : 4 * q + 4, :].bitcast(I32),
             )
-        for q in range(QUADS):
-            nc.scalar.dma_start(
+
+        def load_w_scales(q):
+            nc.sync.dma_start(
                 w_scales[32 * q : 32 * q + 4, :, :].bitcast(I32),
                 w4_scales[:, 4 * q : 4 * q + 4, :].rearrange("a r n -> r a n").bitcast(I32),
             )
-        nc.scalar.dma_start(w_words[:].bitcast(I32), w4_words.rearrange("a p c -> p a c").bitcast(I32))
+
         with nc.allow_non_contiguous_dma(reason="one bias value a partition"):
             nc.scalar.dma_start(b_col[:], b.rearrange("(p o) -> p o", o=1))
-        nc.sync.dma_start(x_sb[0][2][:], x_planes[0, 2])
-        nc.sync.dma_start(x_sb[0][3][:], x_planes[0, 3])
-        u_passes = u.rearrange("(a p i) n -> a p (i n)", p=P, i=PACK)
-        for i in range(PACK):
-            nc.sync.dma_start(x_sb[1][i][:], x_planes[1, i])
-            if i < V_PASSES:
-                nc.sync.dma_start(u_sb[i][:].rearrange("p i n -> p (i n)"), u_passes[i])
-        for a in range(V_PASSES):
-            nc.sync.dma_start(v_words[a][:], tab[a, 0 : PACK * P * T].rearrange("(p c) -> p c", p=P).bitcast(I32))
+        nc.sync.dma_start(list_x[:], offs2)
+        nc.sync.dma_start(wgt_sb[:], wgt)
+        load_x(0, 0)
+        nc.sync.dma_start(list_v[:], offs)
+        for i in range(1, PACK):
+            load_x(0, i)
+            load_v_scales(i - 1)
+        load_x(1, 0)
+        load_v_scales(3)
+        load_u(0)
+        load_x(1, 1)
+        nc.sync.dma_start(w_words[:].bitcast(I32), w4_words.rearrange("a p c -> p a c").bitcast(I32))
+        load_u(1)
+        load_w_scales(0)
+        load_w_scales(1)
+        load_x(1, 2)
+        load_w_scales(2)
+        load_w_scales(3)
+        load_x(1, 3)
+        load_v(0)
+        load_v(1)
+        load_u(2)
+        load_v(2)
 
         acc = [ps.tile([P, M], F32, name=f"acc{t}") for t in range(ROW_TILES)]
-
-        x_codes = []
-        x_scales = []
-        wovens = []
-
-        def quantize_x(a, tag):
-            codes = sb.tile([P, S], U32, name=f"x_codes{a}", tag=tag, align_bytes=64)
-            scales = sb.tile([P, S], U8, name=f"x_scales{a}", align_bytes=64)
-            nc.vector.quantize_mx(out=codes[:].bitcast(FP8X4), scales=scales[:], in_=wovens[a][:].rearrange("p j i -> p (j i)"))
-            x_codes.append(codes)
-            x_scales.append(scales)
-
-        for a in range(X_PASSES):
-            picked = sb.tile([P, PACK, S], F32, name=f"picked{a}")
-            for i in range(PACK):
-                nc.vector.tensor_tensor(picked[:, i, :], x_sb[a][i][:].indirect(list_x[:]), wgt_sb[:], MULT)
-            woven = sb.tile([P, S, PACK], BF16, name=f"woven{a}", align_bytes=64)
-            nc.scalar.copy(
-                woven[:].rearrange("p (c e) i -> p c i e", e=4),
-                picked[:].rearrange("p i (c e) -> p c i e", e=4),
-            )
-            wovens.append(woven)
-            if a == 0:
-                quantize_x(a, "x_codes0")
 
         b_ps = ps.tile([P, M], F32, name="b_ps")
         nc.tensor.transpose(b_ps[:], b_col[:].to_broadcast([P, P]), ident[:])
         b_rows = sb.tile([P, M], F32, name="b_rows")
-        nc.scalar.copy(b_rows[:], b_ps[:])
+        nc.scalar.activation(b_rows[:], b_ps[:], COPY)
 
-        u_woven = sb.tile([P, V_PASSES, M, PACK], BF16, name="u_woven", align_bytes=64)
-        u_codes = sb.tile([P, V_PASSES, M], U32, name="u_codes", align_bytes=64)
-        u_scales = sb.tile([P, V_PASSES, M], U8, name="u_scales", align_bytes=64)
-        for a in range(V_PASSES):
-            nc.scalar.copy(
-                u_woven[:, a].rearrange("p (c e) i -> p c i e", e=4),
-                u_sb[a][:].rearrange("p i (c e) -> p c i e", e=4),
-            )
-        for lo, hi in ((0, 2), (2, 3)):
-            nc.vector.quantize_mx(
-                out=u_codes[:, lo:hi, :].rearrange("p a n -> p (a n)").bitcast(FP8X4),
-                scales=u_scales[:, lo:hi, :].rearrange("p a n -> p (a n)"),
-                in_=u_woven[:, lo:hi].rearrange("p a n i -> p (a n i)"),
-            )
+        def weave(dst, src):
+            nc.scalar.copy(dst.rearrange("p (c e) i -> p c i e", e=4), src.rearrange("p i (c e) -> p c i e", e=4))
 
-        g_scales = sb.tile([P, S], U8, name="g_scales", align_bytes=64)
+        def quantize(codes, scales, woven):
+            nc.vector.quantize_mx(out=codes.bitcast(FP8X4), scales=scales, in_=woven.rearrange("p j i -> p (j i)"))
+
+        picked = [sb.tile([P, PACK, S], F32, name=f"picked{a}") for a in range(X_PASSES)]
+        x_woven = [sb.tile([P, S, PACK], BF16, name=f"x_woven{a}", align_bytes=64) for a in range(X_PASSES)]
+        x_scales = [sb.tile([P, S], U8, name=f"x_scales{a}", align_bytes=64) for a in range(X_PASSES)]
+        u_woven = [sb.tile([P, M, PACK], BF16, name=f"u_woven{a}", tag=f"u_woven{a}", align_bytes=64) for a in range(V_PASSES)]
+        u_codes = [sb.tile([P, M], U32, name=f"u_codes{a}", align_bytes=64) for a in range(V_PASSES)]
+        u_scales = [sb.tile([P, M], U8, name=f"u_scales{a}", align_bytes=64) for a in range(V_PASSES)]
+
+        def pick(a):
+            for i in range(PACK):
+                nc.vector.tensor_tensor(picked[a][:, i, :], x_sb[a][i][:].indirect(list_x[:]), wgt_sb[:], MULT)
+
+        def prepare_u(a):
+            weave(u_woven[a][:], u_sb[a][:])
+            quantize(u_codes[a][:], u_scales[a][:], u_woven[a][:])
+
+        pick(0)
+        weave(x_woven[0][:], picked[0][:])
+        g_scales = sb.tile([P, S], U8, name="g_scales", tag="x_sb0_3", align_bytes=64)
         nc.vector.tensor_copy(g_scales[:], v_scales[:].indirect(list_v[:]))
-        g_words = [sb.tile([P, S], U32, name=f"g_words{a}", align_bytes=64) for a in range(V_PASSES)]
-        for a in range(V_PASSES - 1):
-            nc.vector.tensor_copy(g_words[a][:], v_words[a][:].bitcast(U32).indirect(list_v[:]))
-        quantize_x(1, "v_words1")
-        last = V_PASSES - 1
+        x_codes = [sb.tile([P, S], U32, name="x_codes0", align_bytes=64)]
+        quantize(x_codes[0][:], x_scales[0][:], x_woven[0][:])
+        pick(1)
+        prepare_u(0)
+        prepare_u(1)
         for t in range(ROW_TILES):
-            nc.vector.tensor_copy(
-                g_words[last][:, P * t : P * (t + 1)],
-                v_words[last][:].bitcast(U32).indirect(list_v[:, 8 * t : 8 * (t + 1)]),
-            )
+            rows = slice(P * t, P * (t + 1))
+            weave(x_woven[1][:, rows, :], picked[1][:, :, rows])
+
+        last = V_PASSES - 1
+        g_words = [sb.tile([P, S], U32, name=f"g_words{a}", align_bytes=64) for a in range(last)]
+        for a in range(last):
+            nc.vector.tensor_copy(g_words[a][:], v_words[a][:].bitcast(U32).indirect(list_v[:]))
+        x_codes.append(sb.tile([P, S], U32, name="x_codes1", tag="v_words1", align_bytes=64))
+        for t in range(ROW_TILES):
+            rows = slice(P * t, P * (t + 1))
+            quantize(x_codes[1][:, rows], x_scales[1][:, rows], x_woven[1][:, rows, :])
+
+        def gather_last(dst, t):
+            nc.vector.tensor_copy(dst, v_words[last][:].bitcast(U32).indirect(list_v[:, 8 * t : 8 * (t + 1)]))
+
+        g_first = sb.tile([P, 2 * P], U32, name="g_first", align_bytes=64)
+        gather_last(g_first[:, 0:P], 0)
+        gather_last(g_first[:, P : 2 * P], 1)
+        prepare_u(last)
+        g_second = sb.tile([P, 2 * P], U32, name="g_second", tag=f"u_woven{last}", align_bytes=64)
+        gather_last(g_second[:, 0:P], 2)
+        gather_last(g_second[:, P : 2 * P], 3)
+
+        def v_codes(a, t):
+            if a < last:
+                return g_words[a][:, P * t : P * (t + 1)]
+            half = g_first if t < 2 else g_second
+            return half[:, P * (t % 2) : P * (t % 2 + 1)]
 
         def x_pass(a, start):
             for t in range(ROW_TILES):
@@ -156,10 +185,10 @@ def tile_list_htab_tm_gelu_kernel(tc, xT, w4_words, w4_scales, tab, u, wgt, b, o
                 rows = slice(P * t, P * (t + 1))
                 nc.tensor.matmul_mx(
                     out=acc[t][:],
-                    lhsT=g_words[a][:, rows].bitcast(FP8X4),
+                    lhsT=v_codes(a, t).bitcast(FP8X4),
                     lhsT_scale=g_scales[4 * a : P, rows],
-                    rhs=u_codes[:, a, :].bitcast(FP8X4),
-                    rhs_scale=u_scales[:, a, :],
+                    rhs=u_codes[a][:].bitcast(FP8X4),
+                    rhs_scale=u_scales[a][:],
                     start=False,
                     stop=(a == last),
                 )

from contextlib import ExitStack

import concourse.mybir as mybir
from concourse.masks import make_identity

K, L, M, T, S = 1024, 1536, 128, 1024, 512
FLOPS = 2 * S * M * (K + L)

F32 = mybir.dt.float32
BF16 = mybir.dt.bfloat16
I32 = mybir.dt.int32
U32 = mybir.dt.uint32
U16 = mybir.dt.uint16
U8 = mybir.dt.uint8
FP8X4 = mybir.dt.float8_e4m3fn_x4
FP4X4 = mybir.dt.float4_e2m1fn_x4
MULT = mybir.AluOpType.mult
ADD = mybir.AluOpType.add
COPY = mybir.ActivationFunctionType.Copy
GELU = mybir.ActivationFunctionType.Gelu_apprx_tanh

P = 128
PACK = 4
X_PASSES = K // (P * PACK)
V_PASSES = L // (P * PACK)
ROW_TILES = S // P
QUADS = 4


def tile_list_htab_tm_gelu_kernel(tc, xT, w4_words, w4_scales, tab, u, wgt, b, offs, offs2, out):
    nc = tc.nc
    with ExitStack() as ctx:
        sb = ctx.enter_context(tc.tile_pool(name="sb", bufs=1))
        ps = ctx.enter_context(tc.psum_pool(name="ps", bufs=1))

        list_v = sb.tile([P, S // 16], U16, name="list_v")
        list_x = sb.tile([P, S // 16], U16, name="list_x")
        wgt_sb = sb.tile([P, S], F32, name="wgt_sb")
        x_sb = [[sb.tile([P, T], F32, name=f"x_sb{a}_{i}", tag=f"x_sb{a}_{i}", align_bytes=64) for i in range(PACK)] for a in range(X_PASSES)]
        v_words = [sb.tile([P, T], I32, name=f"v_words{a}", tag=f"v_words{a}", align_bytes=64) for a in range(V_PASSES)]
        v_scales = sb.tile([P, T], U8, name="v_scales")
        w_words = sb.tile([P, X_PASSES, 2 * M], U8, name="w_words", align_bytes=64)
        w_scales = sb.tile([P, X_PASSES, M], U8, name="w_scales", align_bytes=64)
        u_sb = [sb.tile([P, PACK, M], F32, name=f"u_sb{a}") for a in range(V_PASSES)]
        b_col = sb.tile([P, 1], F32, name="b_col")
        ident = sb.tile([P, P], F32, name="ident")

        make_identity(nc, ident[:])
        nc.vector.memset(v_scales[:].bitcast(I32), 0)
        nc.vector.memset(w_scales[:].rearrange("p a n -> p (a n)").bitcast(I32), 0)

        x_planes = xT.rearrange("(a p i) t -> a i p t", p=P, i=PACK)
        tab_scales = tab[:, PACK * P * T :].rearrange("a (q t) -> a q t", t=T)
        u_passes = u.rearrange("(a p i) n -> a p (i n)", p=P, i=PACK)

        def load_u(a):
            nc.sync.dma_start(u_sb[a][:].rearrange("p i n -> p (i n)"), u_passes[a])

        def load_v(a):
            nc.sync.dma_start(v_words[a][:], tab[a, 0 : PACK * P * T].rearrange("(p c) -> p c", p=P).bitcast(I32))

        def load_x(a, i):
            nc.sync.dma_start(x_sb[a][i][:], x_planes[a, i])

        def load_v_scales(q):
            nc.sync.dma_start(
                v_scales[32 * q : 32 * q + 4 * V_PASSES, :].bitcast(I32),
                tab_scales[:, 4 * q : 4 * q + 4, :].bitcast(I32),
            )

        def load_w_scales(q):
            nc.sync.dma_start(
                w_scales[32 * q : 32 * q + 4, :, :].bitcast(I32),
                w4_scales[:, 4 * q : 4 * q + 4, :].rearrange("a r n -> r a n").bitcast(I32),
            )

        with nc.allow_non_contiguous_dma(reason="one bias value a partition"):
            nc.scalar.dma_start(b_col[:], b.rearrange("(p o) -> p o", o=1))
        nc.sync.dma_start(list_x[:], offs2)
        nc.sync.dma_start(wgt_sb[:], wgt)
        load_x(0, 0)
        nc.sync.dma_start(list_v[:], offs)
        for i in range(1, PACK):
            load_x(0, i)
            load_v_scales(i - 1)
        load_x(1, 0)
        load_v_scales(3)
        load_u(0)
        load_x(1, 1)
        nc.sync.dma_start(w_words[:].bitcast(I32), w4_words.rearrange("a p c -> p a c").bitcast(I32))
        load_u(1)
        load_w_scales(0)
        load_w_scales(1)
        load_x(1, 2)
        load_w_scales(2)
        load_w_scales(3)
        load_x(1, 3)
        load_v(0)
        load_v(1)
        load_u(2)
        load_v(2)

        acc = [ps.tile([P, M], F32, name=f"acc{t}") for t in range(ROW_TILES)]

        b_ps = ps.tile([P, M], F32, name="b_ps")
        nc.tensor.transpose(b_ps[:], b_col[:].to_broadcast([P, P]), ident[:])
        b_rows = sb.tile([P, M], F32, name="b_rows")
        nc.scalar.activation(b_rows[:], b_ps[:], COPY)

        def weave(dst, src):
            nc.scalar.copy(dst.rearrange("p (c e) i -> p c i e", e=4), src.rearrange("p i (c e) -> p c i e", e=4))

        def quantize(codes, scales, woven):
            nc.vector.quantize_mx(out=codes.bitcast(FP8X4), scales=scales, in_=woven.rearrange("p j i -> p (j i)"))

        picked = [sb.tile([P, PACK, S], F32, name=f"picked{a}") for a in range(X_PASSES)]
        x_woven = [sb.tile([P, S, PACK], BF16, name=f"x_woven{a}", align_bytes=64) for a in range(X_PASSES)]
        x_scales = [sb.tile([P, S], U8, name=f"x_scales{a}", align_bytes=64) for a in range(X_PASSES)]
        u_woven = [sb.tile([P, M, PACK], BF16, name=f"u_woven{a}", tag=f"u_woven{a}", align_bytes=64) for a in range(V_PASSES)]
        u_codes = [sb.tile([P, M], U32, name=f"u_codes{a}", align_bytes=64) for a in range(V_PASSES)]
        u_scales = [sb.tile([P, M], U8, name=f"u_scales{a}", align_bytes=64) for a in range(V_PASSES)]

        def pick(a):
            for i in range(PACK):
                nc.vector.tensor_tensor(picked[a][:, i, :], x_sb[a][i][:].indirect(list_x[:]), wgt_sb[:], MULT)

        def prepare_u(a):
            weave(u_woven[a][:], u_sb[a][:])
            quantize(u_codes[a][:], u_scales[a][:], u_woven[a][:])

        pick(0)
        weave(x_woven[0][:], picked[0][:])
        g_scales = sb.tile([P, S], U8, name="g_scales", tag="x_sb0_3", align_bytes=64)
        nc.vector.tensor_copy(g_scales[:], v_scales[:].indirect(list_v[:]))
        x_codes = [sb.tile([P, S], U32, name="x_codes0", align_bytes=64)]
        quantize(x_codes[0][:], x_scales[0][:], x_woven[0][:])
        pick(1)
        prepare_u(0)
        prepare_u(1)
        for t in range(ROW_TILES):
            rows = slice(P * t, P * (t + 1))
            weave(x_woven[1][:, rows, :], picked[1][:, :, rows])

        last = V_PASSES - 1
        g_words = [sb.tile([P, S], U32, name=f"g_words{a}", align_bytes=64) for a in range(last)]
        for a in range(last):
            nc.vector.tensor_copy(g_words[a][:], v_words[a][:].bitcast(U32).indirect(list_v[:]))
        x_codes.append(sb.tile([P, S], U32, name="x_codes1", tag="v_words1", align_bytes=64))
        for t in range(ROW_TILES):
            rows = slice(P * t, P * (t + 1))
            quantize(x_codes[1][:, rows], x_scales[1][:, rows], x_woven[1][:, rows, :])

        def gather_last(dst, t):
            nc.vector.tensor_copy(dst, v_words[last][:].bitcast(U32).indirect(list_v[:, 8 * t : 8 * (t + 1)]))

        g_first = sb.tile([P, 2 * P], U32, name="g_first", align_bytes=64)
        gather_last(g_first[:, 0:P], 0)
        gather_last(g_first[:, P : 2 * P], 1)
        prepare_u(last)
        g_second = sb.tile([P, 2 * P], U32, name="g_second", tag=f"u_woven{last}", align_bytes=64)
        gather_last(g_second[:, 0:P], 2)
        gather_last(g_second[:, P : 2 * P], 3)

        def v_codes(a, t):
            if a < last:
                return g_words[a][:, P * t : P * (t + 1)]
            half = g_first if t < 2 else g_second
            return half[:, P * (t % 2) : P * (t % 2 + 1)]

        def x_pass(a, start):
            for t in range(ROW_TILES):
                rows = slice(P * t, P * (t + 1))
                nc.tensor.matmul_mx(
                    out=acc[t][:],
                    lhsT=x_codes[a][:, rows].bitcast(FP8X4),
                    lhsT_scale=x_scales[a][:, rows],
                    rhs=w_words[:, a, :].bitcast(FP4X4),
                    rhs_scale=w_scales[:, a, :],
                    start=start,
                    stop=False,
                )

        def v_pass(a):
            for t in range(ROW_TILES):
                rows = slice(P * t, P * (t + 1))
                nc.tensor.matmul_mx(
                    out=acc[t][:],
                    lhsT=v_codes(a, t).bitcast(FP8X4),
                    lhsT_scale=g_scales[4 * a : P, rows],
                    rhs=u_codes[a][:].bitcast(FP8X4),
                    rhs_scale=u_scales[a][:],
                    start=False,
                    stop=(a == last),
                )

        x_pass(0, True)
        v_pass(0)
        v_pass(1)
        x_pass(1, False)
        v_pass(2)

        for t in range(ROW_TILES):
            summed = sb.tile([P, M], F32, name=f"summed{t}")
            nc.vector.tensor_tensor(summed[:], acc[t][:], b_rows[:], ADD)
            result = sb.tile([P, M], F32, name=f"result{t}")
            nc.scalar.activation(result[:], summed[:], GELU)
            nc.sync.dma_start(out[P * t : P * (t + 1), :], result[:])
